import numpy as np, ml_dtypes
CORES = [40,64,80,88,96,104,120,144]
N = 8
BF = ml_dtypes.bfloat16
def gentries(a):
    return np.ascontiguousarray(a.reshape(8, 16, -1).transpose(0, 2, 1)).reshape(8, -1)
def gtable(e):
    e = np.asarray(e); return np.ascontiguousarray(e.reshape(8, -1, 16).transpose(0, 2, 1)).reshape(128, -1).astype(np.int32)
V, A, K, DB, DP, EP = 1664, 64, 2, 5, 32, 2
RI, GI, G8 = np.arange(N)[:, None, None], np.arange(8)[None, :, None], np.arange(8)[:, None]
def pick(a, i):
    return a[RI, GI, i]
def tall(x):
    return np.ascontiguousarray(x.astype(np.float32).reshape(N, 8, 16, V).transpose(0, 1, 3, 2)).astype(np.int32)
def depths(par):
    j = np.reshape(par, (-1, V)).astype(np.int64); t = np.zeros(j.shape, np.int64) + np.arange(V); n = np.zeros(j.shape, np.int64)
    for _ in range(DP):
        n += t >= A; t = np.take_along_axis(j, t, 1)
    return n.reshape(np.shape(par))
def forest(rng, m, power):
    n = V - A; lev = np.minimum(1 + np.floor(m * rng.random(n) ** power).astype(np.int64), m); lev[rng.permutation(n)[:m]] = np.arange(1, m + 1)
    p = np.arange(V); o = A + np.argsort(lev, kind="stable"); cnt = np.bincount(lev, minlength=m + 1); before = np.arange(A); a = 0
    for l in range(1, m + 1):
        now = o[a:a + cnt[l]]; p[now] = before[rng.integers(0, before.size, now.size)]; before = now; a += cnt[l]
    return p
def parts(rng, deep, power):
    hf = 1 - 2 * rng.integers(0, 2, (N, 128, V)); bt = rng.integers(0, 256, (N, 128, V)); dr = rng.integers(0, 256, (N, 128, V))
    par = np.stack([np.stack([forest(rng, int(deep[r, g]), float(power[r, g])) for g in range(8)]) for r in range(N)])
    return hf, bt, dr, par, rng.integers(0, V, (N, 8, K, V)), rng.integers(0, V, (N, 8, A))
def pack(hf, bt, dr, par, nb, up):
    return {"hf": hf.astype(np.float32).astype(BF), "bt": bt.astype(np.float32).astype(BF), "dr": dr.astype(np.float32).astype(BF), "par": par.astype(np.int32),
            "nb": np.stack([gtable(a.reshape(8, -1)) for a in nb]), "up": np.stack([gtable(a) for a in up])}
def setup_inputs(rng):
    deep = rng.choice(np.array([DP - 1, DP // 2 + 1, DP // 2, DP // 4]), (N, 8)); deep[:, rng.integers(0, 8)] = DP - 1; deep[0, 0] = DP - 1
    return pack(*parts(rng, deep, rng.choice(np.array([0.5, 1.0, 1.5]), (N, 8))))
def setup_inputs_deep(rng):
    hf, bt, dr, par, nb, up = parts(rng, np.full((N, 8), DP - 1), rng.choice(np.array([0.1, 0.25]), (N, 8)))
    o = np.argsort(-depths(par), axis=-1, kind="stable")[:, :, :A]
    for r in range(1, N): up[r] = rng.permuted(o[r - 1], axis=-1)
    hf[:, 16:32] = 1; hf[0, 16:24, :A] = -1; bt[:, 16:32] = 255; dr[:, 16:32] = 0; nb[:, 1] = np.arange(V)
    return pack(hf, bt, dr, par, nb, up)
def setup_inputs_ties(rng):
    hf, bt, dr, par, nb, up = parts(rng, rng.choice(np.array([DP - 1, DP // 2, 5]), (N, 8)), np.full((N, 8), 1.0))
    bt = (bt >> 6) * 64; dr = (dr >> 6) * 64; h4, b4, d4 = hf.reshape(N, 8, 16, V), bt.reshape(N, 8, 16, V), dr.reshape(N, 8, 16, V)
    h4[:, ::2] = h4[:, ::2, :1]; b4[:, ::2] = (b4[:, ::2, :1] >> 7) * 128; d4[:, ::2] = (d4[:, ::2, :1] >> 7) * 128
    nb[:, :, 1:] = np.where(rng.random((N, 8, K - 1, V)) < 0.2, nb[:, :, :1], nb[:, :, 1:]); nb = np.where(rng.random(nb.shape) < 0.1, np.arange(V), nb)
    return pack(hf, bt, dr, par, nb, up)
def setup_inputs_flat(rng):
    deep = np.full((N, 8), DP // 2); deep[:, 0] = 1; deep[:, 1] = 2; deep[:, 2] = DP - 1
    hf, bt, dr, par, nb, up = parts(rng, deep, np.full((N, 8), 1.0)); dep = depths(par); v = np.arange(V); hf[:, 64:80] = 1
    for r in range(N):
        par[r, 1] = np.where(dep[r, 1] == 2, np.flatnonzero(dep[r, 1] == 1)[0], par[r, 1])
        ch = np.arange(V); ch[par[r, 7, A:]] = np.arange(A, V); nb[r, 7, 0] = ch
        c = np.where(v < A, v, 2 * rng.integers(0, A // 2, V) + dep[r, 4] % 2); c = np.where((v >= A) & (c == par[r, 4]), (c + 2) % A, c)
        w = bt[r, 64:80, :A][:, c]; bt[r, 64:80, A:] = (w - w[:, par[r, 4]])[:, A:] & 255; nb[r, 4, r % K] = c
    nb[:, 2] = np.arange(V); hf[:, 48:64] = -1; bt[:, 48:64] = 255; dr[:, 48:64] = 255; up[:, 4] = V - 1; up[:, 5] = rng.integers(0, A, (N, A))
    up[:, 6] = rng.choice(np.array([0, V - 1]), (N, A)); nb[:, 6] = rng.choice(np.array([0, A - 1, A, V - 1]), (N, K, V))
    return pack(hf, bt, dr, par, nb, up)
def setup_inputs_spread(rng):
    hf, bt, dr, par, nb, up = parts(rng, rng.integers(1, DP, (N, 8)), rng.choice(np.array([0.2, 1.0, 4.0]), (N, 8)))
    share = rng.choice(np.array([0.02, 0.3, 0.5, 0.98]), (N, 8, 1, 1)); hf = np.where(rng.random((N, 8, 16, V)) < share, -1, 1).reshape(N, 128, V)
    k = lambda: rng.integers(0, 9, (N, 1, V)); bt = (bt >> k()) * (rng.random((N, 1, V)) > 0.0625); dr = (dr >> k()) * (rng.random((N, 1, V)) > 0.0625)
    nb = np.minimum((V * rng.random(nb.shape) ** 3).astype(np.int64), V - 1); up = np.minimum((V * rng.random(up.shape) ** 3).astype(np.int64), V - 1)
    return pack(hf, bt, dr, par, nb, up)
def check_inputs(d):
    bad = []
    if not np.all(np.abs(d["hf"].astype(np.float32)) == 1): bad.append("hf is 1 or -1")
    for k in ("bt", "dr"):
        x = d[k].astype(np.float32)
        if not np.all((x >= 0) & (x <= 255) & (x == np.floor(x))): bad.append("range of " + k)
    for k in ("par", "nb", "up"):
        if np.min(d[k]) < 0 or np.max(d[k]) > V - 1: bad.append("range of " + k)
    if "range of par" not in bad:
        if np.any(d["par"][:, :, :A] != np.arange(A)): bad.append("an anchor is its own parent")
        if np.max(depths(d["par"])) >= DP: bad.append("depth")
    return bad
def reference(hf, bt, dr, par, nb, up):
    h, b, d = tall(hf), tall(bt), tall(dr); g = np.where(d >= 128, -1, 1).astype(np.int32); move = np.arange(V) >= A
    p = par.astype(np.int64); nl = np.stack([gentries(a) for a in nb]).astype(np.int64).reshape(N, 8, K, V); ul = np.stack([gentries(a) for a in up]).astype(np.int64)
    for e in range(EP):
        Hm = h.copy(); Zm = b.copy(); Hm[:, :, :A] = 1; Zm[:, :, :A] = 0
        j = p; dep = np.broadcast_to(move, p.shape).astype(np.int64)
        for _ in range(DB):
            hp = pick(Hm, j); Zm = hp * Zm + pick(Zm, j); Hm = hp * Hm; dep = dep + pick(dep, j); j = pick(j, j)
        H = np.empty_like(Hm); Z = np.empty_like(Zm)
        for r in range(N):
            ah, az = h[r, :, :A], b[r, :, :A]
            if r > 0:
                uh = H[r - 1][G8, ul[r]]; az = uh * az + Z[r - 1][G8, ul[r]]; ah = uh * ah
            ch = ah[G8, j[r]]; H[r] = ch * Hm[r]; Z[r] = (ch * Zm[r] + az[G8, j[r]]) & 255
        best = np.add.reduce(np.abs(Z - pick(Z, p)), axis=3); new = p
        for k in range(K):
            c = pick(p, nl[:, :, k]); s = np.add.reduce(np.abs(Z - pick(Z, c)), axis=3)
            ok = (pick(dep, c) < dep) & (s < best)
            new = np.where(ok, c, new); best = np.where(ok, s, best)
        p = new
        if e < EP - 1:
            hp = pick(H, p); zb = (hp * (Z - pick(Z, p)) + d) & 255; m = move[:, None]
            h = np.where(m, g * hp * H, h); b = np.where(m, zb, b)
    return {"yx": np.ascontiguousarray(Z.transpose(0, 1, 3, 2)).reshape(N, 128, V).astype(np.float32).astype(BF), "yp": p.astype(np.float32)}

from concourse.bass import DstId, RemoteDMATransfer
from concourse.mybir import AluOpType as ALU, ActivationFunctionType as ACT

V, A, VR, C = 1664, 64, 1728, 104
BF, F32, I32, U16 = "bfloat16", "float32", "int32", "uint16"
MW = (68, 64)
KQ = 49152.0
KS = 2
SD = "gsgg"
ZD = "gsgs"
SLOTS = (1, 2, 2, 0, 0, 2, 1, 2)

SCRATCH = {}
for _n in ("hfb", "btb", "drb", "W", "CW0", "CW1", "SG", "SX", "HA", "YQ", "ZC", "ZP", "AP", "DC", "G0", "D0", "D1", "D2", "ZT",
           "T0", "T1"):
    SCRATCH[_n] = ("sbuf", [128, V], BF)
for _n in ("J0", "J1", "J2", "J3", "J4", "J5", "S0", "S1"):
    SCRATCH[_n] = ("sbuf", [128, VR], BF)
for _n in ("Z0", "Z1", "Z2"):
    SCRATCH[_n] = ("sbuf", [128, VR], F32)
for _n in ("XP", "Y0", "Y1"):
    SCRATCH[_n] = ("sbuf", [128, V], F32)
for _n in ("L0", "L1", "L2", "L3", "L4", "LR", "LP", "LS"):
    SCRATCH[_n] = ("sbuf", [128, C], U16)
for _n, _w, _d in (("X0", C, I32), ("NI", C, I32), ("KI", C, I32), ("HI", 2 * C, I32), ("HL", 2 * C, BF), ("nbi", 2 * C, I32),
                   ("LN", 2 * C, U16), ("LC", 200, U16), ("upi", 4, I32), ("upn", 4, I32), ("uph", 4, I32), ("LU", 32, U16),
                   ("LI", 28, U16), ("MJ", 144, BF), ("MD", 144, BF), ("MS", 144, BF), ("MC", 144, BF), ("one", 128, BF),
                   ("c16", 8, BF), ("c8k", 8, BF), ("t8", 8, BF), ("u8", 8, BF), ("ID", 128, BF), ("NID", 128, BF), ("I128", 128, BF),
                   ("IF", 128, F32), ("pi", 8, I32), ("pj", 8, I32), ("pm", 8, F32), ("m0", 8, F32), ("m1", 8, F32), ("m2", 8, F32),
                   ("m3", 8, F32), ("ia", A, BF), ("ic", C, F32), ("i4", 8, F32), ("I104", 128, BF), ("JG", 256, BF),
                   ("ZG", 512, F32), ("yq", A, BF), ("gu", A, BF), ("zu", A, BF), ("tu", A, BF), ("rz", A, BF),
                   ("qa", A, F32), ("qb", A, F32), ("DA", 2 * C, F32), ("DV", 2 * C, F32), ("CE", 2 * C, F32),
                   ("EK", 2 * C, F32), ("EP", C, F32), ("ka", C, F32), ("kb", C, F32), ("YP", C, F32)):
    SCRATCH[_n] = ("sbuf", [128, _w], _d)
for _i in range(4):
    SCRATCH["msg%d" % _i] = ("sbuf", [128, MW[_i % 2]], BF)
    SCRATCH["hm%d" % _i] = ("sbuf", [128, MW[_i % 2]], BF)
    SCRATCH["lnk%d" % _i] = ("sbuf", [128, 7, MW[_i % 2]], BF)
for _n in ("P0", "P1", "P2", "P3", "Q0", "Q1", "Q2", "Q3"):
    SCRATCH[_n] = ("psum", [128, 512], F32)
PSUM = ("P0", "P1", "P2", "P3", "Q0", "Q1", "Q2", "Q3")
NDMA = 16
SEMAPHORES = ["cv", "cs", "cp", "cg", "aup", "hup", "al0", "al1", "ah0", "ah1", "ah2", "ah3", "loc"] + ["d%d" % _i for _i in range(NDMA)]


def bits(engines):
    m = 0
    for e in engines:
        m |= 1 << e
    return m


def routes(T, topo):
    cores, out = T.cores, []
    for r, c in enumerate(cores):
        later = list(range(r + 1, len(cores)))
        direct = [s for s in later if topo.may_write(c, cores[s])]
        relay = [s for s in later if s not in direct]
        able = [h for h in topo.cores_of(c) if T.rank_of(h) is None and all(topo.may_write(h, x) for x in cores)]
        far = [h for h in able if topo.die(h) != topo.die(c)]
        near = [h for h in able if topo.die(h) == topo.die(c)]
        hs = [far[0], near[0]]
        if len(relay) >= 3:
            k = (len(relay) + 1) // 2
            helpers = [(hs[0], relay[len(relay) - k:]), (hs[1], relay[:len(relay) - k])]
        elif relay:
            helpers = [(hs[0], relay)]
        else:
            helpers = []
        uph = hs[0] if r > 0 and not topo.may_write(c, cores[r - 1]) else None
        out.append({"direct": direct, "helpers": helpers, "uph": uph})
    return out


def dst_of(topo, d, s):
    rid, pid = topo.addr(d, s)
    return DstId(rid=rid, pnc=pid)


def helper_program(g, core, T, topo, rt):
    cores, sent = T.cores, 0
    for r, c in enumerate(cores):
        if rt[r]["uph"] == core:
            g.wait_ge(T.sem.hup, len(topo.engines(c, core)))
            rid, pid = topo.addr(cores[r - 1], core)
            g.remote_dma(T.upn[:], T.uph[:], T.sem.aup, T.sem.loc, pid, rid, topo.mask(core, cores[r - 1]))
            sent += len(topo.engines(core, cores[r - 1]))
        for h, dests in rt[r]["helpers"]:
            if h != core:
                continue
            for m in range(4):
                g.wait_ge(T.sem["ah%d" % m], len(helper_engines(T, topo, rt, r, h)))
                g.remote_dma_fused([RemoteDMATransfer(
                    dst_ids=[dst_of(topo, cores[s], core) for s in dests], dma_engine_mask=topo.mask(core, cores[dests[0]]),
                    remote_sem=T.sem["al%d" % (m // 2)], srcs=[T["hm%d" % m][:]],
                    dsts=[T["lnk%d" % m][:, r, :] for s in dests])], local_sem=T.sem.loc)
                sent += len(topo.engines(core, cores[dests[0]]))
    if sent:
        g.wait_ge(T.sem.loc, sent)


def helper_engines(T, topo, rt, r, h):
    c = T.cores[r]
    off = topo.engines(c, T.cores[rt[r]["direct"][0]]) if rt[r]["direct"] else []
    free = [e for e in topo.engines(c, h) if e not in off]
    hs = [x for x, _ in rt[r]["helpers"]]
    n = len(free) // len(hs)
    k = hs.index(h)
    return free[k * n:(k + 1) * n]


def arrivals(T, topo, rt, s):
    n = 0
    for r in range(s):
        if s in rt[r]["direct"]:
            n += len(topo.engines(T.cores[r], T.cores[s]))
        for h, dests in rt[r]["helpers"]:
            if s in dests:
                n += len(topo.engines(h, T.cores[s]))
    return n


def emit(g, T, ops):
    queue = {"v": g.vector, "s": g.scalar, "p": g.tensor, "g": g, "y": g.sync}
    seen, deps = {}, []
    for i, o in enumerate(ops):
        mine = set()
        for wr, regs in ((False, o["r"]), (True, o["w"])):
            for (name, lo, hi, row) in regs:
                for (j, jw, jlo, jhi, jrow) in seen.get(name, []):
                    p = ops[j]
                    same = p["q"] == o["q"] and p["sig"] is None and o["sig"] is None
                    meet = lo < jhi and jlo < hi and (row is None or jrow is None or row == jrow) and (wr or jw)
                    if same:
                        if o["q"] != "p" and meet:
                            mine.add(j)
                    elif name in PSUM or meet:
                        mine.add(j)
        for wr, regs in ((False, o["r"]), (True, o["w"])):
            for (name, lo, hi, row) in regs:
                seen.setdefault(name, []).append((i, wr, lo, hi, row))
        deps.append(mine)
    need, upto, clock, marked = [], {}, [], set()
    for i, o in enumerate(ops):
        known, ws = upto.setdefault(o["q"], {}), []
        for j in sorted(deps[i], reverse=True):
            key = ops[j]["q"] if ops[j]["sig"] is None else j
            if known.get(key, -1) < j:
                ws.append(j)
                if ops[j]["sig"] is None:
                    marked.add(j)
                for kk, vv in clock[j].items():
                    known[kk] = max(known.get(kk, -1), vv)
        need.append(sorted(ws))
        clock.append(dict(known))
        clock[i][o["q"] if o["sig"] is None else i] = i
    count, val = {}, {}
    for i, o in enumerate(ops):
        if i in marked:
            count[o["q"]] = count.get(o["q"], 0) + 1
            val[i] = ("c" + o["q"], count[o["q"]])
        elif o["sig"] is not None:
            val[i] = o["sig"]
    waited = set()
    for i, o in enumerate(ops):
        if o["f"] is None:
            continue
        q = queue[o["q"]]
        for j in need[i]:
            q.wait_ge(T.sem[val[j][0]], val[j][1])
            waited.add(j)
        ins = o["f"](q)
        if o["dma"]:
            ins.then_inc(T.sem[o["sig"][0]], 16)
        elif i in marked:
            ins.then_inc(T.sem[val[i][0]], 1)
    for i, o in enumerate(ops):
        if o["sig"] is not None and i not in waited:
            queue["g" if o["f"] is None else o["q"]].wait_ge(T.sem[o["sig"][0]], o["sig"][1])


def rank_program(g, core, T, topo):
    rt = routes(T, topo)
    rank = T.rank_of(core)
    if rank is None:
        helper_program(g, core, T, topo, rt)
        return
    N = len(T.cores)
    sends, takes = rank < N - 1, rank > 0
    ops, nd, sent = [], [0], [0]

    def a(name, lo=0, hi=None, step=1):
        hi = SCRATCH[name][1][-1] if hi is None else hi
        ap = T[name][:, lo:hi] if step == 1 else T[name][:, lo:hi:step]
        return (ap, [(name, lo, hi, None)])

    def col(name):
        return a(name, 0, 1)

    def row(name, q):
        return (T[name][q::16, 0:V], [(name, 0, V, q)])

    def ind(win, width, off, lo, hi):
        return (T[win][:, 0:width].indirect(T[off][:, lo:hi]), [(win, 0, width, None), (off, lo, hi, None)])

    def op(q, f, reads, writes, sig=None, dma=False):
        ops.append({"q": q, "f": f, "r": [x for o in reads for x in o[1]], "w": [x for o in writes for x in o[1]],
                    "sig": sig, "dma": dma})

    def dma(q, out, in_):
        s = "d%d" % nd[0]
        nd[0] += 1
        op(q, lambda e: e.dma_start(out[0], in_[0]), [in_], [out], (s, 16), True)

    def hbm(ap):
        return (ap, [])

    def bare(s):
        return s[0] if isinstance(s, tuple) else s

    def tt(out, x, y, o):
        op("v", lambda e: e.tensor_tensor(out[0], x[0], y[0], o), [x, y], [out])

    def ts(out, x, s1, o0, s2=None, o1=None):
        rd = [x] + [s for s in (s1, s2) if isinstance(s, tuple)]
        if o1 is None:
            op("v", lambda e: e.tensor_scalar(out[0], x[0], bare(s1), None, o0), rd, [out])
        else:
            op("v", lambda e: e.tensor_scalar(out[0], x[0], bare(s1), bare(s2), o0, o1), rd, [out])

    def cp(out, x):
        op("v", lambda e: e.tensor_copy(out[0], x[0]), [x], [out])

    def ms(out, c):
        op("v", lambda e: e.memset(out[0], c), [], [out])

    def act(out, x, f, bias=None, scale=None):
        rd = [x] + [s for s in (bias, scale) if isinstance(s, tuple)]
        kw = {}
        if bias is not None:
            kw["bias"] = bare(bias)
        if scale is not None:
            kw["scale"] = bare(scale)
        op("s", lambda e: e.activation(out[0], x[0], f, **kw), rd, [out])

    def mm(out, l, r, start, stop):
        op("p", lambda e: e.matmul(out[0], l[0], r[0], start, stop), [l, r], [out])

    def iota(out, pat, base, cm, whole=False):
        if whole:
            op("g", lambda e: e.iota(out[0], pat, base, cm), [], [out])
        else:
            op("g", lambda e: e.iota(out[0], pat, base, cm, allow_small_or_imprecise_dtypes=True), [], [out])

    def sel(out, x, pat, cmp, fill, base, cm):
        op("g", lambda e: e.affine_select(out[0], x[0], pat, cmp, fill, base, cm), [x], [out])

    def twin(q, out, src, lo, hi):
        if q == "g":
            sel(a(out, lo, hi), a(src, lo, hi), [[1, hi - lo]], ALU.is_ge, 0.0, 0, 0)
        elif q == "s":
            act(a(out, lo, hi), a(src, lo, hi), ACT.Copy)
        else:
            cp(a(out, lo, hi), a(src, lo, hi))

    def conv(M, src, c0, c1, Q, off):
        for i in range(16):
            mm(a(Q, off, off + c1 - c0), a(M, 15 - i, 143 - i), a(src, 16 * c0 + i, 16 * c1, 16), i == 0, i == 15)

    def convx(M, src, Q, off, i0=0, i1=16):
        for i in range(i0, i1):
            mm(a(Q, off, off + C), a(M, 15 - i, 143 - i), a(src, C * i, C * i + C), i == 0, i == 15)

    CH = ((4, 54), (54, C))
    C4 = ((4, 30), (30, 54), (54, 80), (80, C))
    N4 = [(16 * c0, 16 * c1) for (c0, c1) in C4]
    A4 = [(416 * j, 416 * j + 416) for j in range(4)]
    SB, TB = ("S0", "S1"), ("T0", "T1")
    ZB, YB = ("Z0", "Z1", "Z2"), ("Y0", "Y1")
    four = range(4)

    def passes(chunks, js, terms, start, stop):
        for j in js:
            (lo, hi) = chunks[j]
            for k, (M, src) in enumerate(terms):
                mm(a("P%d" % j, 0, hi - lo), a(M), a(src, lo, hi), start and k == 0, stop and k == len(terms) - 1)

    def bank(j):
        return a("P%d" % j, 0, N4[j][1] - N4[j][0])

    def roots(out):
        act(out, a("ia"), ACT.Identity, bias=col("m0"), scale=col("m1"))

    dma("y", a("X0"), hbm(T.par[:]))
    if takes:
        dma("s", a("upi"), hbm(T.up[:]))
    dma("y", a("hfb"), hbm(T.hf[:]))
    dma("y", a("nbi"), hbm(T.nb[:]))
    ms(a("one"), 1.0)
    ms(a("c16"), 16.0)
    ms(a("MJ"), 0.0)
    iota(col("pi"), [[0, 1]], 0, 1, True)
    iota(a("ia"), [[1, A]], 0, 0)
    sel(a("t8"), a("c16"), [[-16, 8]], ALU.is_equal, 0.0, 0, 1)
    sel(a("MJ", 15, 128, 16), a("t8"), [[-16, 8]], ALU.not_equal, 1.0, -1, 1)
    iota(a("ic"), [[1, C]], 0, 0)
    iota(a("i4", 0, 4), [[16, 4]], 0, 0)
    sel(a("ID"), a("one"), [[-1, 128]], ALU.is_equal, 0.0, 0, 1)
    ts(col("pj"), col("pi"), 15, ALU.bitwise_and)
    ms(a("J0"), 0.0)
    cp(col("pm"), col("pj"))
    for b in SB:
        act(a(b, V, VR), a("one", 0, A), ACT.Copy)
    for b in ZB:
        act(a(b, V, VR), a("one", 0, A), ACT.Copy, scale=0.0)
    for b in ("D0", "D1", "D2", "CW0", "CW1"):
        act(a(b, 0, A), a("one", 0, A), ACT.Copy, scale=0.0)
    act(a("G0", 0, A), a("one", 0, A), ACT.Copy, scale=2.0)
    ts(col("m1"), col("pm"), 1.0, ALU.is_equal)
    ts(col("m3"), col("pm"), 3.0, ALU.subtract, col("pm"), ALU.mult)
    ts(col("m2"), col("pm"), 104.0, ALU.mult)
    ts(col("m0"), col("m3"), 0.0, ALU.is_equal, 104.0, ALU.mult)
    ts(a("HI", 0, C), a("X0"), 4, ALU.arith_shift_right)
    ts(a("HI", C, 2 * C), a("X0"), 15, ALU.bitwise_and)
    cp(a("HL"), a("HI"))
    roots(a("J1", 0, A))
    roots(a("J1", V, VR))
    dma("y", row("J0", 0), a("HL", 0, C))
    dma("s", row("J0", 1), a("HL", C, 2 * C))
    if takes:
        h = rt[rank]["uph"]
        to = T.cores[rank - 1] if h is None else h
        rid, pid = topo.addr(to, core)
        sent[0] += len(topo.engines(core, to))
        land, sem = (T.upn[:], T.sem.aup) if h is None else (T.uph[:], T.sem.hup)
        op("g", lambda e: e.remote_dma(land, T.upi[:], sem, T.sem.loc, pid, rid, topo.mask(core, to)), [a("upi")], [])
    for k in range(2, 5):
        roots(a("J%d" % k, 0, A))
        roots(a("J%d" % k, V, VR))
    act(a("W", 0, A), a("ia"), ACT.Copy, scale=col("m1"))
    act(a("NID"), a("ID"), ACT.Copy, scale=-1.0)
    act(a("I128"), a("ID"), ACT.Copy, scale=128.0)
    act(a("IF"), a("ID"), ACT.Copy)
    act(a("I104"), a("ID"), ACT.Copy, scale=104.0)
    dma("y", a("btb"), hbm(T.bt[:]))
    dma("y", a("drb"), hbm(T.dr[:]))
    for b in ("MD", "MS", "MC"):
        iota(a(b), [[0, 144]], 0, 0)
    iota(a("c8k"), [[0, 8]], 8192, 0)
    sel(a("MD", 15, 128, 16), a("one", 0, 8), [[-16, 8]], ALU.is_equal, 0.0, -2, 1)
    sel(a("u8"), a("c8k"), [[-16, 8]], ALU.is_ge, 0.0, 0, 1)
    sel(a("MS", 15, 128, 16), a("u8"), [[16, 8]], ALU.is_ge, 0.0, 15, -1)
    sel(a("MC", 15, 128, 16), a("MJ", 15, 128, 16), [[-16, 8]], ALU.not_equal, -16.0, -3, 1)
    ts(a("LS"), a("ic"), col("m2"), ALU.add)
    ts(a("LR", 0, 4), a("i4", 0, 4), col("pm"), ALU.add)
    ts(a("NI", 0, 4), a("i4", 0, 4), col("pm"), ALU.add, float(V), ALU.add)
    if not takes:
        ms(a("qa"), KQ)
    cp(a("LN"), a("nbi"))
    ts(a("S0", A, V), a("hfb", A, V), 0.5, ALU.mult)
    for b in SB:
        act(a(b, 0, A), a("hfb", 0, A), ACT.Copy)
    roots(a("J0", 0, A))
    act(a("T0", 864, V), a("hfb", 864, V), ACT.Copy, scale=0.5)
    for j, (c0, c1) in enumerate(CH):
        conv("MJ", "J0", c0, c1, "Q%d" % j, 0)
    ts(a("T0", A, 864), a("hfb", A, 864), 0.5, ALU.mult)
    cp(a("L0", 4, 54), a("Q0", 0, 50))

    def link_step(e, n):
        if not sends:
            return
        if n == 0:
            act(a("JG", 0, 64), ind("J4", VR, "LU", 0, 4), ACT.Copy)
            conv("MJ", "JG", 0, 4, "Q2", 0)
        elif n == 1:
            cp(a("LU", 4, 8), a("Q2", 0, 4))
        elif n == 2:
            act(a("JG", 0, 128), ind("J3", VR, "LU", 0, 8), ACT.Copy)
            act(a("JG", 128, 192), ind("J4", VR, "LU", 4, 8), ACT.Copy)
            conv("MJ", "JG", 0, 12, "Q2", 0)
        elif n == 3:
            cp(a("LU", 8, 16), a("Q2", 0, 8))
            ts(a("msg%d" % (2 * e), A, A + 4), a("Q2", 8, 12), -float(V), ALU.add)
        elif n == 4:
            act(a("JG"), ind("J2", VR, "LU", 0, 16), ACT.Copy)
            conv("MJ", "JG", 0, 16, "Q2", 0)
        elif n == 5:
            cp(a("LU", 16, 32), a("Q2", 0, 16))

    def send(m):
        msg, tr = T["msg%d" % m], []
        d = rt[rank]["direct"]
        if d:
            tr.append(RemoteDMATransfer(
                dst_ids=[dst_of(topo, T.cores[s], core) for s in d], dma_engine_mask=topo.mask(core, T.cores[d[0]]),
                remote_sem=T.sem["al%d" % (m // 2)], srcs=[msg[:]], dsts=[T["lnk%d" % m][:, rank, :] for s in d]))
            sent[0] += len(topo.engines(core, T.cores[d[0]]))
        for h, _ in rt[rank]["helpers"]:
            en = helper_engines(T, topo, rt, rank, h)
            tr.append(RemoteDMATransfer(dst_ids=[dst_of(topo, h, core)], dma_engine_mask=bits(en), remote_sem=T.sem["ah%d" % m],
                                        srcs=[msg[:]], dsts=[T["hm%d" % m][:]]))
            sent[0] += len(en)
        op("g", lambda q: q.remote_dma_fused(tr, local_sem=T.sem.loc), [a("msg%d" % m)], [])

    for e in range(2):
        mh, mz = "msg%d" % (2 * e), "msg%d" % (2 * e + 1)
        n = C if e else 100
        WIN, MP = ("W", "MJ") if e else ("J0", "MC")
        for k in range(5):
            src, dst, L = SB[k % 2], SB[(k + 1) % 2], "L%d" % k
            for j, (c0, c1) in enumerate(C4):
                lo, hi = 16 * c0, 16 * c1
                if k < 4 and j % 2 == 0:
                    (d0, d1) = CH[j // 2]
                    if k == 0:
                        act(a("J1", 16 * d0, 16 * d1), ind("J0", V, "LP" if e else "L0", d0, d1), ACT.Copy)
                    else:
                        act(a("J%d" % (k + 1), 16 * d0, 16 * d1), ind("J%d" % k, VR, L, d0, d1), ACT.Copy)
                    conv("MJ", "J%d" % (k + 1), d0, d1, "Q%d" % (j // 2), 0)
                    b = 2 * k + j // 2 - 3
                    if 0 <= b < 4:
                        if e == 0:
                            passes(N4, [b], [("ID", "btb"), ("I128", "hfb")], True, True)
                        else:
                            passes(N4, [b], [("ID", "AP")], False, False)
                    if j == 2 and SD[1] == "s":
                        twin("s", TB[(k + 1) % 2], dst, N4[1][0], N4[1][1])
                if k == 4 and j == 0:
                    link_step(e, 0)
                    if e == 0:
                        for jj in four:
                            act(bank(jj), bank(jj), ACT.Abs, bias=-128.0)
                    else:
                        act(a("ZP", A, 864), ind("ZC", V, "L0", 4, 54), ACT.Copy)
                        passes(N4, (0, 1), [("NID", "ZP")], False, True)
                if k == 4 and j == 2:
                    if e == 1:
                        act(a("ZP", 864, V), ind("ZC", V, "L0", 54, C), ACT.Copy)
                        passes(N4, (2, 3), [("NID", "ZP")], False, True)
                    for jj in range(2):
                        act(a("SG", N4[jj][0] if jj else 0, N4[jj][1]), a(dst, N4[jj][0] if jj else 0, N4[jj][1]), ACT.Sign)
                tt(a(dst, lo, hi), ind(src, VR, L, c0, c1), a(TB[k % 2], lo, hi), ALU.mult)
                if k == 4 and j >= 2:
                    act(a("SG", lo, hi), a(dst, lo, hi), ACT.Sign)
                if e == 0 and k == 0 and j == 0:
                    cp(a("L0", 54, C), a("Q1", 0, 50))
                if k < 4 and SD[j] == "g":
                    twin("g", TB[(k + 1) % 2], dst, lo, hi)
                if k < 4 and j % 2:
                    (d0, d1) = CH[j // 2]
                    cp(a("L%d" % (k + 1), d0, d1), a("Q%d" % (j // 2), 0, d1 - d0))
                if k < 4 and SD[j] == "v":
                    twin("v", TB[(k + 1) % 2], dst, lo, hi)
                if k == 4 and j == 1:
                    link_step(e, 1)
                if e == 0 and k == 2 and j == 3 and sends:
                    h = rt[rank + 1]["uph"]
                    op("x", None, [], [a("upn")], ("aup", len(topo.engines(T.cores[rank + 1] if h is None else h, core))))
                    cp(a("LU", 0, 4), a("upn"))
        for b in ZB:
            act(a(b, 0, A), a("ZC" if e else "btb", 0, A), ACT.Copy)
        for j, (lo, hi) in enumerate(N4):
            tt(a("Z0", lo, hi), bank(j), a("SG", lo, hi), ALU.mult)
            twin(ZD[j], "Y0", "Z0", lo, hi)
            if j == 0:
                link_step(e, 2)
        if sends:
            if e == 0:
                act(a(mh, 0, A), ind("S1", VR, "LU", 0, 4), ACT.Sign)
            else:
                act(a("gu"), ind("G0", V, "LU", 0, 4), ACT.Copy)
                act(a("zu"), ind("ZC", V, "LU", 0, 4), ACT.Copy)
        if e == 0:
            dma("y", row(WIN, 2), row("S1", 0))

        def job(kind, m, j):
            (c0, c1) = C4[j]
            lo, hi = 16 * c0, 16 * c1
            if kind == "root":
                act(a("J5", lo, hi), ind("J4", VR, "L4", c0, c1), ACT.Copy)
                if j % 2:
                    conv("MJ", "J5", CH[j // 2][0], CH[j // 2][1], "P0" if e else "Q3", CH[j // 2][0])
            elif kind == "self":
                act(a("W", lo, hi), ind("J0", V, "LS", c0, c1), ACT.Copy)
                if j == 3:
                    dma("y", row("W", 2), row("S1", 0))
            elif kind == "flip":
                act(a("G0", lo, hi), a("drb", lo, hi), ACT.Sign, bias=127.5, scale=-1.0)
                passes(N4, [j], [("ID", "drb"), ("I128", "G0")], True, True)
            elif kind == "step":
                act(a("DC", lo, hi), bank(j), ACT.Identity, bias=-128.0)
            else:
                cw = "CW%d" % m
                act(a(cw, lo, hi), ind(WIN, V, "LN", C * m + c0, C * m + c1), ACT.Copy)
                if j == 3 and m == 0:
                    if e == 0:
                        conv(MP, WIN, 4, C, "Q0", 2 * n)
                        conv("MD", WIN, 4, C, "Q1", 2 * n)
                    else:
                        convx(MP, WIN, "Q0", 2 * n)
                        convx("MD", WIN, "Q1", 2 * n)
                if j == 3:
                    if e == 0:
                        conv(MP, cw, 4, C, "Q0", n * m)
                        conv("MD", cw, 4, C, "Q1", n * m)
                    else:
                        conv(MP, cw, 4, C, "Q3", 100 * m)
                        convx(MP, cw, "Q0", n * m)
                        convx("MD", cw, "Q1", n * m)

        if e == 0:
            jobs = [("root", 0, j) for j in four] + [("cand", m, j) for m in range(2) for j in four]
            jobs += [("flip", 0, j) for j in four] + [("step", 0, j) for j in four]
        else:
            jobs = [("self", 0, j) for j in four] + [("root", 0, j) for j in four] + [("cand", m, j) for m in range(2) for j in four]
        for k in range(5):
            src, dst = ZB[k % 3], ZB[(k + 1) % 3]
            if k == KS and sends:
                t = 32 >> KS
                for m in range(t):
                    if m % 4 == 0:
                        act(a("ZG", 64 * m, 64 * m + 256), ind(src, VR, "LU", 4 * m, 4 * m + 16), ACT.Identity, bias=KQ / t)
                    mm(a("Q2", 64, 128), a("IF"), a("ZG", 64 * m, 64 * m + 64), m == 0, e == 0 and m == t - 1)
                if e == 1:
                    mm(a("Q2", 64, 128), a("NID"), a("rz"), False, True)
            if k == 4:
                while jobs:
                    job(*jobs.pop(0))
            for j, (c0, c1) in enumerate(C4 if k < 4 else CH):
                lo, hi = 16 * c0, 16 * c1
                tt(a(dst, lo, hi), ind(src, VR, "L%d" % k, c0, c1), a(YB[k % 2], lo, hi), ALU.add)
                if k < 4:
                    twin(ZD[j], YB[(k + 1) % 2], dst, lo, hi)
                if k == KS and sends and j == 1:
                    act(a("yq"), a("Q2", 64, 128), ACT.Copy)
                if k == KS and sends and j == 3:
                    tt(a(mz), a("Q2", 64, 128), a("yq"), ALU.subtract)
                    send(2 * e + 1)
                if k < 4 and j % 2:
                    for _ in range(SLOTS[2 * k + j // 2]):
                        job(*jobs.pop(0))
                if k == 0 and j == 0 and e == 1 and sends:
                    tt(a("tu"), ind("S1", VR, "LU", 0, 4), a("gu"), ALU.mult)
                    act(a(mh, 0, A), a("tu"), ACT.Sign)
                if k == 0 and j == 0 and sends:
                    link_step(e, 3)
                    send(2 * e)
                    link_step(e, 4)
                if k == 1 and j == 0:
                    link_step(e, 5)
            if k == 0 and e == 1 and sends:
                tt(a("rz"), a(mh, 0, A), a("zu"), ALU.mult)
        ts(a("LR", 4, C), a("P0" if e else "Q3", 4, C), -float(V), ALU.add)
        if takes:
            lh, lz = T["lnk%d" % (2 * e)], T["lnk%d" % (2 * e + 1)]
            whole = [("lnk%d" % e, 0, 1, None)]
            op("x", None, [], [(None, whole)], ("al%d" % e, 2 * arrivals(T, topo, rt, rank)))
            ts(a("qb"), (lz[:, 0, :], whole), KQ, ALU.add)
            if rank > 1:
                cp(a("LI", 4, 4 * rank), (lh[:, 1:rank, A:A + 4], whole))
            tt(a("qa"), a("qb"), (lh[:, 0, 0:A], whole), ALU.mult)
            for r in range(1, rank):
                tt(a("qb"), ind("qa", A, "LI", 4 * r, 4 * r + 4), (lz[:, r, :], whole), ALU.add)
                tt(a("qa"), a("qb"), (lh[:, r, 0:A], whole), ALU.mult)
        for j, (lo, hi) in enumerate(A4):
            tt(a("XP", lo, hi), ind("qa", A, "LR", 26 * j, 26 * j + 26), a("Z2", lo, hi), ALU.add)
            act(a("P%d" % j, 0, 416), a("XP", lo, hi), ACT.Abs)
            for jj in ([j - 1] if j else []) + ([j] if j == 3 else []):
                act(a("YQ", A4[jj][0], A4[jj][1]), a("P%d" % jj, 0, 416), ACT.Identity, bias=-127.5)
        cp(a("LC"), a("Q3" if e else "Q0", 0, 200))
        for j, (lo, hi) in enumerate(A4):
            tt(a("ZC", lo, hi), a("P%d" % j, 0, 416), a("YQ", lo, hi), ALU.subtract)
            twin("gsgg"[j], "ZT", "ZC", lo, hi)
            if e == 1 and j % 2:
                dma("y", hbm(T.yx[:, lo - 416:hi]), a("ZC", lo - 416, hi))
        act(a("DA", 0, 2 * n), a("Q1", 0, 2 * n), ACT.Abs)
        for m in range(2):
            act(a("DV", n * m, n * m + n), a("Q1", 2 * n, 3 * n), ACT.Abs)
            act(a("CE", n * m, n * m + n), a("Q0", n * m, n * m + n), ACT.Identity, bias=float(2048 * (m + 1) - 2 ** 24))
        act(a("EP", 0, n), a("Q0", 2 * n, 3 * n), ACT.Identity, bias=-float(2 ** 24))
        banks, x = ("Q0", "Q1", "Q3"), 0
        for m in range(3):
            D, done = "D%d" % m, 0
            for (c0, c1) in (((4, 52), (52, C)) if m < 2 else ((4, 54), (54, 86), (86, C))):
                lo, hi = 16 * c0, 16 * c1
                lst = ind("ZC", V, "L0", c0, c1) if m == 0 else ind("ZC", V, "LC", 100 * (m - 1) + c0 - 4, 100 * (m - 1) + c1 - 4)
                tt(a(D, lo, hi), lst, a("ZT", lo, hi), ALU.subtract)
                act(a(D, lo, hi), a(D, lo, hi), ACT.Abs)
                if e == 0:
                    if c1 == C or x == 4:
                        conv("MS", D, 4 + done, c1, banks[m], done)
                        done = c1 - 4
                    if x < 4:
                        act(a("SX", A4[x][0], A4[x][1]), a("XP", A4[x][0], A4[x][1]), ACT.Sign)
                        passes(A4, [x], [("ID", "SG"), ("ID", "SX")], True, True)
                else:
                    convx("MS", D, banks[m], 0, done, hi // C)
                    done = hi // C
                if x == 0:
                    tt(a("DV", 0, 2 * n), a("DV", 0, 2 * n), a("DA", 0, 2 * n), ALU.subtract)
                    act(a("DA", 0, 2 * n), a("DV", 0, 2 * n), ACT.Relu, scale=float(2 ** 57))
                if x == 2:
                    tt(a("EK", 0, 2 * n), a("DA", 0, 2 * n), a("CE", 0, 2 * n), ALU.add)
                if x == 3:
                    tt(a("ka", 0, n), a("Q0", 0, n), a("EP", 0, n), ALU.add)
                if x == 5:
                    tt(a("kb", 0, n), a("Q1", 0, n), a("EK", 0, n), ALU.add)
                x += 1
        tt(a("ka", 0, n), a("ka", 0, n), a("kb", 0, n), ALU.min)
        if e == 0:
            for j, (lo, hi) in enumerate(A4):
                act(a("HA", lo, hi), a("P%d" % j, 0, 416), ACT.Abs)
            passes(N4, four, [("ID", "ZC"), ("NID", "DC")], True, False)
            for b in SB:
                act(a(b, 0, A), a("one", 0, A), ACT.Copy)
        tt(a("kb", 0, n), a("Q3", 0, n), a("EK", n, 2 * n), ALU.add)
        tt(a("KI", 0, n), a("ka", 0, n), a("kb", 0, n), ALU.min)
        if e == 0:
            ts(a("NI", 4, C), a("KI", 0, n), 2047, ALU.bitwise_and)
            cp(a("L0", 4, C), a("NI", 4, C))
            for j, (lo, hi) in enumerate(N4):
                act(a("S0", lo, hi), ind("G0", V, "L0", C4[j][0], C4[j][1]), ACT.Copy, scale=0.5)
                if j < 3:
                    twin("g", "T0", "S0", lo, hi)
            ts(a("HI", 0, C), a("NI"), 4, ALU.arith_shift_right)
            ts(a("HI", C, 2 * C), a("NI"), 15, ALU.bitwise_and)
            cp(a("HL"), a("HI"))
            dma("y", row("J0", 0), a("HL", 0, C))
            dma("y", row("J0", 1), a("HL", C, 2 * C))
            mm(a("Q2", 0, C), a("I104"), a("HL", C, 2 * C), True, False)
            mm(a("Q2", 0, C), a("ID"), a("HL", 0, C), False, True)
            tt(a("AP", A, 864), ind("HA", V, "L0", 4, 54), a("DC", A, 864), ALU.mult)
            cp(a("LP"), a("Q2", 0, C))
            tt(a("AP", 864, V), ind("HA", V, "L0", 54, C), a("DC", 864, V), ALU.mult)
            twin("v", "T0", "S0", N4[3][0], N4[3][1])
        else:
            ts(a("NI"), a("KI"), 2047, ALU.bitwise_and)
            cp(a("YP"), a("NI"))
            dma("y", hbm(T.yp[:]), a("YP"))
    emit(g, T, ops)
    if sent[0]:
        g.wait_ge(T.sem.loc, sent[0])
